import numpy as np
import ml_dtypes


def mxq(x, axis, fmt="e4m3"):
    dtype, down = {"e4m3": (ml_dtypes.float8_e4m3fn, 7), "e5m2": (ml_dtypes.float8_e5m2, 14)}[fmt]
    v = np.moveaxis(np.asarray(x, np.float32).astype(ml_dtypes.bfloat16).astype(np.float64), axis, -1)
    blocks = v.reshape(v.shape[:-1] + (-1, 32))
    amax = np.abs(blocks).max(-1, keepdims=True)
    byte = np.maximum(np.where(amax > 0, np.frexp(amax)[1] - 1 + 127, 0) - down, 1)
    scale = np.exp2(byte - 127.0)
    codes = (blocks / scale).astype(np.float32).astype(dtype).astype(np.float64)
    return np.moveaxis((codes * scale).reshape(v.shape), -1, axis)


WIDE = False


def mx_kscale(k):
    if not WIDE:
        return np.ones(k)
    levels = np.array([10, -10, 5, -5, 0])
    if k % 512:
        return np.exp2(np.random.permutation(np.resize(levels, k // 32))).repeat(32)
    a = np.empty((k // 512, 16))
    for p in range(k // 512):
        a[p, :8] = np.random.permutation(np.resize(levels, 8))
        for g in range(8):
            far = levels[np.abs(levels - a[p, g]) >= 10]
            a[p, g + 8] = far[np.random.randint(len(far))]
    return np.exp2(a.ravel()).repeat(32)


def f64(x):
    return np.asarray(x).astype(np.float64)


def striped8(idx):
    return np.concatenate([v.reshape(-1, 16).T for v in idx]).astype(np.uint16)


def unstriped8(offs):
    return np.stack([offs[16 * g:16 * g + 16].T.reshape(-1) for g in range(8)]).astype(np.int64)


E2M1 = np.array([0.0, 0.5, 1.0, 1.5, 2.0, 3.0, 4.0, 6.0, -0.0, -0.5, -1.0, -1.5, -2.0, -3.0, -4.0, -6.0])


def pack_weight(w, fmt):
    k, n = w.shape
    w = f64(np.asarray(w, np.float32).astype(ml_dtypes.bfloat16)).reshape(k // 32, 32, n)
    amax = np.abs(w).max(1)
    if fmt == "e4m3":
        byte = np.frexp(amax)[1] - 1 + 127 - 7
    else:
        mant, ex = np.frexp(amax / 6.0)
        byte = np.where(mant > 0.5, ex, ex - 1) + 127
    byte = np.clip(np.where(amax > 0, byte, 1), 1, 254)
    scaled = (w * np.exp2(127.0 - byte)[:, None, :]).reshape(k, n).astype(np.float32)
    by_word = np.ascontiguousarray(scaled.reshape(k // 512, 128, 4, n).transpose(0, 1, 3, 2))
    if fmt == "e4m3":
        words = by_word.astype(ml_dtypes.float8_e4m3fn).view(np.uint8)
    else:
        c = by_word.astype(ml_dtypes.float4_e2m1fn).view(np.uint8) & 0xF
        words = (c[..., 0::2] | (c[..., 1::2] << 4)).reshape(k // 512, 128, 2 * n)
    return np.ascontiguousarray(words), np.ascontiguousarray(byte.astype(np.uint8).reshape(k // 512, 16, n))


def unpack_weight(words, scales, fmt):
    g, _, n = scales.shape
    words = np.ascontiguousarray(words).reshape(g, 128, n, -1)
    if fmt == "e4m3":
        vals = words.view(ml_dtypes.float8_e4m3fn).astype(np.float64)
    else:
        nib = np.empty((g, 128, n, 4), np.uint8)
        nib[..., 0::2] = words & 0xF
        nib[..., 1::2] = words >> 4
        vals = E2M1[nib]
    vals = vals * np.repeat(np.exp2(scales.astype(np.float64) - 127.0), 8, axis=1)[..., None]
    return vals.transpose(0, 1, 3, 2).reshape(g * 512, n)


def gelu(v):
    return 0.5 * v * (1.0 + np.tanh(np.sqrt(2.0 / np.pi) * (v + 0.044715 * v**3)))


K, M, T, S = 2048, 256, 512, 256


def setup_inputs():
    n = np.random.standard_normal
    s = mx_kscale(K)[:, None]
    w = n((K, M)) / np.sqrt(K) / s
    p_w8 = pack_weight(w[:512], "e4m3")
    p_w4 = pack_weight(w[512:], "e2m1")
    return {
        "x": (n((K, S)) * s).astype(np.float32),
        "w8_words": p_w8[0],
        "w8_scales": p_w8[1],
        "w4_words": p_w4[0],
        "w4_scales": p_w4[1],
        "b": (0.3 * n(256)).astype(np.float32),
        "wgo": np.repeat(np.random.uniform(0.5, 2.0, (8, S)), 16, axis=0).astype(np.float32),
        "offs": striped8(np.stack([np.random.permutation(T)[:S] for _ in range(8)])),
    }


def reference(x, w8_words, w8_scales, w4_words, w4_scales, b, wgo, offs):
    x_ = mxq(f64(x), 0, "e4m3")
    w8_ = unpack_weight(w8_words, w8_scales, "e4m3")
    w4_ = unpack_weight(w4_words, w4_scales, "e2m1")
    y = w8_.T @ x_[:512] + w4_.T @ x_[512:]
    place = unstriped8(offs)[np.arange(M) % 128 // 16]
    out = np.zeros((M, T))
    out[np.arange(M)[:, None], place] = f64(wgo)[np.arange(M) % 128] * (gelu(y + f64(b)[:, None]))
    return out

@@ -1,0 +1,169 @@
+from contextlib import ExitStack
+
+import concourse.mybir as mybir
+
+K, M, T, S = 2048, 256, 512, 256
+FLOPS = 2 * K * M * S
+
+F32 = mybir.dt.float32
+BF16 = mybir.dt.bfloat16
+I32 = mybir.dt.int32
+U32 = mybir.dt.uint32
+U16 = mybir.dt.uint16
+U8 = mybir.dt.uint8
+FP8X4 = mybir.dt.float8_e4m3fn_x4
+FP4X4 = mybir.dt.float4_e2m1fn_x4
+GELU = mybir.ActivationFunctionType.Gelu_apprx_tanh
+MULT = mybir.AluOpType.mult
+
+P = 128
+PACK = 4
+K_PASS = P * PACK
+HALF = 128
+PASS_ORDER = (1, 2, 3, 0)
+WHOLE = (1,)
+VCOLS = {(1, 0): 128, (1, 1): 0, (2, 0): 128, (3, 0): 128, (0, 0): 64, (2, 1): 0, (3, 1): 0, (0, 1): 0}
+
+
+def tile_list_hscat_o_gelu_kernel(tc, x, w8_words, w8_scales, w4_words, w4_scales, b, wgo, offs, out):
+    nc = tc.nc
+    with ExitStack() as ctx:
+        keep = ctx.enter_context(tc.tile_pool(name="keep", bufs=1))
+        psum = ctx.enter_context(tc.psum_pool(name="psum", bufs=1))
+
+        offsets = keep.tile([P, S // 16], U16, name="offsets")
+        w8 = keep.tile([P, M], U32, name="w8", align_bytes=64)
+        w4 = keep.tile([P, 3, 2 * M], U8, name="w4", align_bytes=64)
+        s8 = keep.tile([P, M], U8, name="s8", align_bytes=64)
+        s4 = keep.tile([P, 3, M], U8, name="s4", align_bytes=64)
+        rows8 = keep.tile([P, M], U8, name="rows8")
+        rows4 = keep.tile([P, 3, M], U8, name="rows4")
+        bias = keep.tile([P, 2], F32, name="bias")
+        gain = keep.tile([P, S], F32, name="gain")
+        pages = [keep.tile([P, T], F32, name=f"page{m}") for m in range(2)]
+        acc = {(m, h): psum.tile([P, HALF], F32, name=f"acc{m}{h}") for m in range(2) for h in range(2)}
+        raw = {}
+
+        def load_x(a, h):
+            rows = x[a * K_PASS:(a + 1) * K_PASS, :].rearrange("(p t) j -> p t j", t=PACK)
+            if h is None:
+                t = keep.tile([P, PACK, S], F32, name=f"raw{a}")
+                nc.sync.dma_start(out=t[:], in_=rows)
+                for hh in range(2):
+                    raw[(a, hh)] = t[:, :, hh * HALF:(hh + 1) * HALF]
+            else:
+                t = keep.tile([P, PACK, HALF], F32, name=f"raw{a}{h}")
+                nc.sync.dma_start(out=t[:], in_=rows[:, :, h * HALF:(h + 1) * HALF])
+                raw[(a, h)] = t[:]
+
+        def load_w8():
+            nc.sync.dma_start(out=w8[:].bitcast(I32), in_=w8_words[0].rearrange("p n t -> p (n t)").bitcast(I32))
+
+        def load_w4():
+            nc.sync.dma_start(out=w4[:].bitcast(I32), in_=w4_words.rearrange("a p c -> p a c").bitcast(I32))
+
+        def load_s4(eng):
+            for q in range(4):
+                eng.dma_start(out=rows4[32 * q:32 * q + 4, :, :].bitcast(I32),
+                              in_=w4_scales[:, 4 * q:4 * q + 4, :].rearrange("a r n -> r a n").bitcast(I32))
+
+        def load_s8(eng):
+            for q in range(4):
+                eng.dma_start(out=rows8[32 * q:32 * q + 4, :].bitcast(I32),
+                              in_=w8_scales[0, 4 * q:4 * q + 4, :].bitcast(I32))
+
+        def move_scales(plane, rows):
+            for q in range(4):
+                nc.vector.tensor_copy(out=plane[32 * q:32 * q + 4].bitcast(I32), in_=rows[32 * q:32 * q + 4].bitcast(I32))
+
+        def load_two(a):
+            t = keep.tile([P, 2, PACK, S], F32, name=f"raw{a}")
+            nc.sync.dma_start(out=t[:], in_=x[a * K_PASS:(a + 2) * K_PASS, :].rearrange("(a p t) j -> p a t j", a=2, t=PACK))
+            for d in range(2):
+                for hh in range(2):
+                    raw[(a + d, hh)] = t[:, d, :, hh * HALF:(hh + 1) * HALF]
+
+        def load_bias(eng):
+            with nc.allow_non_contiguous_dma(reason="one bias value to a partition"):
+                eng.dma_start(out=bias[:], in_=b.rearrange("(m p) -> p m", p=P))
+
+        def load_gain(eng):
+            eng.dma_start(out=gain[:], in_=wgo)
+
+        def load_offs():
+            nc.sync.dma_start(offsets[:], offs)
+
+        def contract(a, h):
+            grouped = keep.tile([P, HALF, PACK], BF16, name=f"grouped{a}{h}", align_bytes=64)
+            codes = keep.tile([P, HALF], U32, name=f"codes{a}{h}", align_bytes=64)
+            scales = keep.tile([P, HALF], U8, name=f"scales{a}{h}", align_bytes=64)
+            v = VCOLS[(a, h)]
+            src = raw[(a, h)]
+            if v < HALF:
+                nc.scalar.copy(out=grouped[:, v:, :].rearrange("p (c i) t -> p c t i", i=4),
+                               in_=src[:, :, v:].rearrange("p t (c i) -> p c t i", i=4))
+            if v > 0:
+                nc.vector.tensor_copy(out=grouped[:, :v, :].rearrange("p (c i) t -> p c t i", i=4),
+                                      in_=src[:, :, :v].rearrange("p t (c i) -> p c t i", i=4))
+            nc.vector.quantize_mx(out=codes[:].bitcast(FP8X4), scales=scales[:],
+                                  in_=grouped[:].rearrange("p j t -> p (j t)"))
+            for m in range(2):
+                if a == 0:
+                    lhs = w8[:, m * P:(m + 1) * P].bitcast(FP8X4)
+                    lsc = s8[:, m * P:(m + 1) * P]
+                else:
+                    lhs = w4[:, a - 1, 2 * m * P:2 * (m + 1) * P].bitcast(FP4X4)
+                    lsc = s4[:, a - 1, m * P:(m + 1) * P]
+                nc.tensor.matmul_mx(out=acc[(m, h)][:], lhsT=lhs, lhsT_scale=lsc,
+                                    rhs=codes[:].bitcast(FP8X4), rhs_scale=scales[:],
+                                    start=(a == PASS_ORDER[0]), stop=(a == PASS_ORDER[-1]))
+
+        def place(m, h, act=None):
+            if act is None:
+                act = keep.tile([P, HALF], F32, name=f"act{m}{h}")[:]
+            nc.scalar.activation(act, acc[(m, h)][:], GELU, bias=bias[:, m:m + 1])
+            cols = HALF // 16
+            nc.vector.tensor_tensor(pages[m][:].indirect(offsets[:, h * cols:(h + 1) * cols]),
+                                    act, gain[:, h * HALF:(h + 1) * HALF], MULT)
+
+        def store(m, eng):
+            eng.dma_start(out=out[m * P:(m + 1) * P, :], in_=pages[m][:])
+
+        warm = keep.tile([P, 1], F32, name="warm")
+        nc.gpsimd.memset(warm[:], 0.0)
+        load_bias(nc.gpsimd)
+        load_gain(nc.gpsimd)
+        nc.vector.memset(s4[:].bitcast(I32), 0)
+        nc.vector.memset(s8[:].bitcast(I32), 0)
+        for m in range(2):
+            nc.vector.memset(pages[m][:], 0.0)
+        load_s4(nc.scalar)
+        warm2 = keep.tile([P, 1], F32, name="warm2")
+        nc.scalar.activation(warm2[:], warm[:], GELU)
+        load_s8(nc.scalar)
+        load_x(1, None)
+        load_w4()
+        load_x(2, 0)
+        load_x(3, 0)
+        load_x(0, 0)
+        load_w8()
+        load_x(2, 1)
+        load_offs()
+        load_x(3, 1)
+        load_x(0, 1)
+        move_scales(s4, rows4)
+        contract(1, 0)
+        contract(1, 1)
+        contract(2, 0)
+        contract(3, 0)
+        move_scales(s8, rows8)
+        contract(0, 0)
+        place(0, 0)
+        contract(2, 1)
+        contract(3, 1)
+        contract(0, 1)
+        place(1, 0, raw[(0, 1)][:, 0, :])
+        place(0, 1)
+        store(0, nc.sync)
+        place(1, 1)
+        store(1, nc.sync)

@@ -22,7 +22,7 @@ K_PASS = P * PACK
 HALF = 128
 PASS_ORDER = (1, 2, 3, 0)
 WHOLE = (1,)
-VCOLS = {(1, 0): 128, (1, 1): 0, (2, 0): 128, (3, 0): 128, (0, 0): 64, (2, 1): 0, (3, 1): 0, (0, 1): 0}
+VCOLS = {(1, 0): 128, (1, 1): 0, (2, 0): 0, (3, 0): 128, (0, 0): 64, (2, 1): 128, (3, 1): 0, (0, 1): 0}
 
 
 def tile_list_hscat_o_gelu_kernel(tc, x, w8_words, w8_scales, w4_words, w4_scales, b, wgo, offs, out):
@@ -36,13 +36,13 @@ def tile_list_hscat_o_gelu_kernel(tc, x, w8_words, w8_scales, w4_words, w4_scale
         w4 = keep.tile([P, 3, 2 * M], U8, name="w4", align_bytes=64)
         s8 = keep.tile([P, M], U8, name="s8", align_bytes=64)
         s4 = keep.tile([P, 3, M], U8, name="s4", align_bytes=64)
-        rows8 = keep.tile([P, M], U8, name="rows8")
         rows4 = keep.tile([P, 3, M], U8, name="rows4")
         bias = keep.tile([P, 2], F32, name="bias")
         gain = keep.tile([P, S], F32, name="gain")
         pages = [keep.tile([P, T], F32, name=f"page{m}") for m in range(2)]
         acc = {(m, h): psum.tile([P, HALF], F32, name=f"acc{m}{h}") for m in range(2) for h in range(2)}
         raw = {}
+        seen = {}
 
         def load_x(a, h):
             rows = x[a * K_PASS:(a + 1) * K_PASS, :].rearrange("(p t) j -> p t j", t=PACK)
@@ -67,9 +67,9 @@ def tile_list_hscat_o_gelu_kernel(tc, x, w8_words, w8_scales, w4_words, w4_scale
                 eng.dma_start(out=rows4[32 * q:32 * q + 4, :, :].bitcast(I32),
                               in_=w4_scales[:, 4 * q:4 * q + 4, :].rearrange("a r n -> r a n").bitcast(I32))
 
-        def load_s8(eng):
-            for q in range(4):
-                eng.dma_start(out=rows8[32 * q:32 * q + 4, :].bitcast(I32),
+        def load_s8(eng, q):
+            if True:
+                eng.dma_start(out=s8[32 * q:32 * q + 4, :].bitcast(I32),
                               in_=w8_scales[0, 4 * q:4 * q + 4, :].bitcast(I32))
 
         def move_scales(plane, rows):
@@ -107,6 +107,7 @@ def tile_list_hscat_o_gelu_kernel(tc, x, w8_words, w8_scales, w4_words, w4_scale
                                       in_=src[:, :, :v].rearrange("p t (c i) -> p c t i", i=4))
             nc.vector.quantize_mx(out=codes[:].bitcast(FP8X4), scales=scales[:],
                                   in_=grouped[:].rearrange("p j t -> p (j t)"))
+            seen[("q", a, h)] = codes
             for m in range(2):
                 if a == 0:
                     lhs = w8[:, m * P:(m + 1) * P].bitcast(FP8X4)
@@ -122,6 +123,7 @@ def tile_list_hscat_o_gelu_kernel(tc, x, w8_words, w8_scales, w4_words, w4_scale
             if act is None:
                 act = keep.tile([P, HALF], F32, name=f"act{m}{h}")[:]
             nc.scalar.activation(act, acc[(m, h)][:], GELU, bias=bias[:, m:m + 1])
+            seen[("g", m, h)] = act
             cols = HALF // 16
             nc.vector.tensor_tensor(pages[m][:].indirect(offsets[:, h * cols:(h + 1) * cols]),
                                     act, gain[:, h * HALF:(h + 1) * HALF], MULT)
@@ -129,26 +131,29 @@ def tile_list_hscat_o_gelu_kernel(tc, x, w8_words, w8_scales, w4_words, w4_scale
         def store(m, eng):
             eng.dma_start(out=out[m * P:(m + 1) * P, :], in_=pages[m][:])
 
+        nc.gpsimd.memset(s8[:].bitcast(I32), 0)
         warm = keep.tile([P, 1], F32, name="warm")
         nc.gpsimd.memset(warm[:], 0.0)
         load_bias(nc.gpsimd)
         load_gain(nc.gpsimd)
         nc.vector.memset(s4[:].bitcast(I32), 0)
-        nc.vector.memset(s8[:].bitcast(I32), 0)
         for m in range(2):
             nc.vector.memset(pages[m][:], 0.0)
         load_s4(nc.scalar)
         warm2 = keep.tile([P, 1], F32, name="warm2")
         nc.scalar.activation(warm2[:], warm[:], GELU)
-        load_s8(nc.scalar)
+        load_offs()
         load_x(1, None)
         load_w4()
         load_x(2, 0)
         load_x(3, 0)
+        load_s8(nc.sync, 0)
         load_x(0, 0)
+        load_s8(nc.sync, 1)
         load_w8()
+        load_s8(nc.sync, 2)
         load_x(2, 1)
-        load_offs()
+        load_s8(nc.sync, 3)
         load_x(3, 1)
         load_x(0, 1)
         move_scales(s4, rows4)
@@ -156,7 +161,6 @@ def tile_list_hscat_o_gelu_kernel(tc, x, w8_words, w8_scales, w4_words, w4_scale
         contract(1, 1)
         contract(2, 0)
         contract(3, 0)
-        move_scales(s8, rows8)
         contract(0, 0)
         place(0, 0)
         contract(2, 1)

from contextlib import ExitStack

import concourse.mybir as mybir

K, M, T, S = 2048, 256, 512, 256
FLOPS = 2 * K * M * S

F32 = mybir.dt.float32
BF16 = mybir.dt.bfloat16
I32 = mybir.dt.int32
U32 = mybir.dt.uint32
U16 = mybir.dt.uint16
U8 = mybir.dt.uint8
FP8X4 = mybir.dt.float8_e4m3fn_x4
FP4X4 = mybir.dt.float4_e2m1fn_x4
GELU = mybir.ActivationFunctionType.Gelu_apprx_tanh
MULT = mybir.AluOpType.mult

P = 128
PACK = 4
K_PASS = P * PACK
HALF = 128
PASS_ORDER = (1, 2, 3, 0)
WHOLE = (1,)
VCOLS = {(1, 0): 128, (1, 1): 0, (2, 0): 0, (3, 0): 128, (0, 0): 64, (2, 1): 128, (3, 1): 0, (0, 1): 0}


def tile_list_hscat_o_gelu_kernel(tc, x, w8_words, w8_scales, w4_words, w4_scales, b, wgo, offs, out):
    nc = tc.nc
    with ExitStack() as ctx:
        keep = ctx.enter_context(tc.tile_pool(name="keep", bufs=1))
        psum = ctx.enter_context(tc.psum_pool(name="psum", bufs=1))

        offsets = keep.tile([P, S // 16], U16, name="offsets")
        w8 = keep.tile([P, M], U32, name="w8", align_bytes=64)
        w4 = keep.tile([P, 3, 2 * M], U8, name="w4", align_bytes=64)
        s8 = keep.tile([P, M], U8, name="s8", align_bytes=64)
        s4 = keep.tile([P, 3, M], U8, name="s4", align_bytes=64)
        rows4 = keep.tile([P, 3, M], U8, name="rows4")
        bias = keep.tile([P, 2], F32, name="bias")
        gain = keep.tile([P, S], F32, name="gain")
        pages = [keep.tile([P, T], F32, name=f"page{m}") for m in range(2)]
        acc = {(m, h): psum.tile([P, HALF], F32, name=f"acc{m}{h}") for m in range(2) for h in range(2)}
        raw = {}
        seen = {}

        def load_x(a, h):
            rows = x[a * K_PASS:(a + 1) * K_PASS, :].rearrange("(p t) j -> p t j", t=PACK)
            if h is None:
                t = keep.tile([P, PACK, S], F32, name=f"raw{a}")
                nc.sync.dma_start(out=t[:], in_=rows)
                for hh in range(2):
                    raw[(a, hh)] = t[:, :, hh * HALF:(hh + 1) * HALF]
            else:
                t = keep.tile([P, PACK, HALF], F32, name=f"raw{a}{h}")
                nc.sync.dma_start(out=t[:], in_=rows[:, :, h * HALF:(h + 1) * HALF])
                raw[(a, h)] = t[:]

        def load_w8():
            nc.sync.dma_start(out=w8[:].bitcast(I32), in_=w8_words[0].rearrange("p n t -> p (n t)").bitcast(I32))

        def load_w4():
            nc.sync.dma_start(out=w4[:].bitcast(I32), in_=w4_words.rearrange("a p c -> p a c").bitcast(I32))

        def load_s4(eng):
            for q in range(4):
                eng.dma_start(out=rows4[32 * q:32 * q + 4, :, :].bitcast(I32),
                              in_=w4_scales[:, 4 * q:4 * q + 4, :].rearrange("a r n -> r a n").bitcast(I32))

        def load_s8(eng, q):
            if True:
                eng.dma_start(out=s8[32 * q:32 * q + 4, :].bitcast(I32),
                              in_=w8_scales[0, 4 * q:4 * q + 4, :].bitcast(I32))

        def move_scales(plane, rows):
            for q in range(4):
                nc.vector.tensor_copy(out=plane[32 * q:32 * q + 4].bitcast(I32), in_=rows[32 * q:32 * q + 4].bitcast(I32))

        def load_two(a):
            t = keep.tile([P, 2, PACK, S], F32, name=f"raw{a}")
            nc.sync.dma_start(out=t[:], in_=x[a * K_PASS:(a + 2) * K_PASS, :].rearrange("(a p t) j -> p a t j", a=2, t=PACK))
            for d in range(2):
                for hh in range(2):
                    raw[(a + d, hh)] = t[:, d, :, hh * HALF:(hh + 1) * HALF]

        def load_bias(eng):
            with nc.allow_non_contiguous_dma(reason="one bias value to a partition"):
                eng.dma_start(out=bias[:], in_=b.rearrange("(m p) -> p m", p=P))

        def load_gain(eng):
            eng.dma_start(out=gain[:], in_=wgo)

        def load_offs():
            nc.sync.dma_start(offsets[:], offs)

        def contract(a, h):
            grouped = keep.tile([P, HALF, PACK], BF16, name=f"grouped{a}{h}", align_bytes=64)
            codes = keep.tile([P, HALF], U32, name=f"codes{a}{h}", align_bytes=64)
            scales = keep.tile([P, HALF], U8, name=f"scales{a}{h}", align_bytes=64)
            v = VCOLS[(a, h)]
            src = raw[(a, h)]
            if v < HALF:
                nc.scalar.copy(out=grouped[:, v:, :].rearrange("p (c i) t -> p c t i", i=4),
                               in_=src[:, :, v:].rearrange("p t (c i) -> p c t i", i=4))
            if v > 0:
                nc.vector.tensor_copy(out=grouped[:, :v, :].rearrange("p (c i) t -> p c t i", i=4),
                                      in_=src[:, :, :v].rearrange("p t (c i) -> p c t i", i=4))
            nc.vector.quantize_mx(out=codes[:].bitcast(FP8X4), scales=scales[:],
                                  in_=grouped[:].rearrange("p j t -> p (j t)"))
            seen[("q", a, h)] = codes
            for m in range(2):
                if a == 0:
                    lhs = w8[:, m * P:(m + 1) * P].bitcast(FP8X4)
                    lsc = s8[:, m * P:(m + 1) * P]
                else:
                    lhs = w4[:, a - 1, 2 * m * P:2 * (m + 1) * P].bitcast(FP4X4)
                    lsc = s4[:, a - 1, m * P:(m + 1) * P]
                nc.tensor.matmul_mx(out=acc[(m, h)][:], lhsT=lhs, lhsT_scale=lsc,
                                    rhs=codes[:].bitcast(FP8X4), rhs_scale=scales[:],
                                    start=(a == PASS_ORDER[0]), stop=(a == PASS_ORDER[-1]))

        def place(m, h, act=None):
            if act is None:
                act = keep.tile([P, HALF], F32, name=f"act{m}{h}")[:]
            nc.scalar.activation(act, acc[(m, h)][:], GELU, bias=bias[:, m:m + 1])
            seen[("g", m, h)] = act
            cols = HALF // 16
            nc.vector.tensor_tensor(pages[m][:].indirect(offsets[:, h * cols:(h + 1) * cols]),
                                    act, gain[:, h * HALF:(h + 1) * HALF], MULT)

        def store(m, eng):
            eng.dma_start(out=out[m * P:(m + 1) * P, :], in_=pages[m][:])

        nc.gpsimd.memset(s8[:].bitcast(I32), 0)
        warm = keep.tile([P, 1], F32, name="warm")
        nc.gpsimd.memset(warm[:], 0.0)
        load_bias(nc.gpsimd)
        load_gain(nc.gpsimd)
        nc.vector.memset(s4[:].bitcast(I32), 0)
        for m in range(2):
            nc.vector.memset(pages[m][:], 0.0)
        load_s4(nc.scalar)
        warm2 = keep.tile([P, 1], F32, name="warm2")
        nc.scalar.activation(warm2[:], warm[:], GELU)
        load_offs()
        load_x(1, None)
        load_w4()
        load_x(2, 0)
        load_x(3, 0)
        load_s8(nc.sync, 0)
        load_x(0, 0)
        load_s8(nc.sync, 1)
        load_w8()
        load_s8(nc.sync, 2)
        load_x(2, 1)
        load_s8(nc.sync, 3)
        load_x(3, 1)
        load_x(0, 1)
        move_scales(s4, rows4)
        contract(1, 0)
        contract(1, 1)
        contract(2, 0)
        contract(3, 0)
        contract(0, 0)
        place(0, 0)
        contract(2, 1)
        contract(3, 1)
        contract(0, 1)
        place(1, 0, raw[(0, 1)][:, 0, :])
        place(0, 1)
        store(0, nc.sync)
        place(1, 1)
        store(1, nc.sync)
